import numpy as np
import ml_dtypes


def mxq(x, axis, fmt="e4m3"):
    dtype, down = {"e4m3": (ml_dtypes.float8_e4m3fn, 7), "e5m2": (ml_dtypes.float8_e5m2, 14)}[fmt]
    v = np.moveaxis(np.asarray(x, np.float32).astype(ml_dtypes.bfloat16).astype(np.float64), axis, -1)
    blocks = v.reshape(v.shape[:-1] + (-1, 32))
    amax = np.abs(blocks).max(-1, keepdims=True)
    byte = np.maximum(np.where(amax > 0, np.frexp(amax)[1] - 1 + 127, 0) - down, 1)
    scale = np.exp2(byte - 127.0)
    codes = (blocks / scale).astype(np.float32).astype(dtype).astype(np.float64)
    return np.moveaxis((codes * scale).reshape(v.shape), -1, axis)


WIDE = False


def mx_kscale(k):
    if not WIDE:
        return np.ones(k)
    levels = np.array([10, -10, 5, -5, 0])
    if k % 512:
        return np.exp2(np.random.permutation(np.resize(levels, k // 32))).repeat(32)
    a = np.empty((k // 512, 16))
    for p in range(k // 512):
        a[p, :8] = np.random.permutation(np.resize(levels, 8))
        for g in range(8):
            far = levels[np.abs(levels - a[p, g]) >= 10]
            a[p, g + 8] = far[np.random.randint(len(far))]
    return np.exp2(a.ravel()).repeat(32)


def f64(x):
    return np.asarray(x).astype(np.float64)


def striped(idx):
    return np.tile(idx.reshape(-1, 16).T, (8, 1)).astype(np.uint16)


def unstriped(offs):
    return offs[:16].T.reshape(-1).astype(np.int64)


E2M1 = np.array([0.0, 0.5, 1.0, 1.5, 2.0, 3.0, 4.0, 6.0, -0.0, -0.5, -1.0, -1.5, -2.0, -3.0, -4.0, -6.0])


def pack_weight(w, fmt):
    k, n = w.shape
    w = f64(np.asarray(w, np.float32).astype(ml_dtypes.bfloat16)).reshape(k // 32, 32, n)
    amax = np.abs(w).max(1)
    if fmt == "e4m3":
        byte = np.frexp(amax)[1] - 1 + 127 - 7
    else:
        mant, ex = np.frexp(amax / 6.0)
        byte = np.where(mant > 0.5, ex, ex - 1) + 127
    byte = np.clip(np.where(amax > 0, byte, 1), 1, 254)
    scaled = (w * np.exp2(127.0 - byte)[:, None, :]).reshape(k, n).astype(np.float32)
    by_word = np.ascontiguousarray(scaled.reshape(k // 512, 128, 4, n).transpose(0, 1, 3, 2))
    if fmt == "e4m3":
        words = by_word.astype(ml_dtypes.float8_e4m3fn).view(np.uint8)
    else:
        c = by_word.astype(ml_dtypes.float4_e2m1fn).view(np.uint8) & 0xF
        words = (c[..., 0::2] | (c[..., 1::2] << 4)).reshape(k // 512, 128, 2 * n)
    return np.ascontiguousarray(words), np.ascontiguousarray(byte.astype(np.uint8).reshape(k // 512, 16, n))


def unpack_weight(words, scales, fmt):
    g, _, n = scales.shape
    words = np.ascontiguousarray(words).reshape(g, 128, n, -1)
    if fmt == "e4m3":
        vals = words.view(ml_dtypes.float8_e4m3fn).astype(np.float64)
    else:
        nib = np.empty((g, 128, n, 4), np.uint8)
        nib[..., 0::2] = words & 0xF
        nib[..., 1::2] = words >> 4
        vals = E2M1[nib]
    vals = vals * np.repeat(np.exp2(scales.astype(np.float64) - 127.0), 8, axis=1)[..., None]
    return vals.transpose(0, 1, 3, 2).reshape(g * 512, n)


def gelu(v):
    return 0.5 * v * (1.0 + np.tanh(np.sqrt(2.0 / np.pi) * (v + 0.044715 * v**3)))


K, H, N, T, S, T2, P = 1024, 1024, 512, 2048, 1024, 2048, 512

def setup_inputs():
    n = np.random.standard_normal
    s = mx_kscale(K)[:, None]
    u = mx_kscale(H)[:, None]
    tab_words, tab_scales = pack_weight(n((K, T)) * s, "e4m3")
    w4_words, w4_scales = pack_weight(n((H, N)) / np.sqrt(H) / u, "e2m1")
    perm = np.random.permutation(T2)
    return {
        "tab_words": tab_words, "tab_scales": tab_scales,
        "offs": striped(np.random.permutation(T)[:S]),
        "w1": (1.3 * n((K, H)) / np.sqrt(K) / s).astype(np.float32),
        "bias1": (0.6 * n(H)).astype(np.float32),
        "gain": (1.2 * np.exp(0.3 * n(H)) * u[:, 0]).astype(np.float32),
        "wgs": np.exp(0.3 * n((128, S))).astype(np.float32),
        "page0": (n((H, T2)) * u).astype(np.float32),
        "offs2": striped(np.random.permutation(T2)[:S]),
        "offs3": striped(perm[:P]),
        "offs4": striped(perm[P:2 * P]),
        "w4_words": w4_words, "w4_scales": w4_scales,
        "bias2": (0.6 * n(N)).astype(np.float32),
    }

def reference(tab_words, tab_scales, offs, w1, bias1, gain, wgs, page0, offs2, offs3, offs4, w4_words, w4_scales, bias2):
    v = unpack_weight(tab_words, tab_scales, "e4m3")[:, unstriped(offs)]
    d = mxq(f64(w1), 0, "e4m3").T @ v
    h = np.tanh(d + f64(bias1)[:, None]) * f64(gain)[:, None]
    page = f64(page0).copy()
    page[:, unstriped(offs2)] = np.tile(f64(wgs), (H // 128, 1)) * h
    a = page[:, unstriped(offs3)]
    b = page[:, unstriped(offs4)]
    page[:, unstriped(offs3)] = np.maximum(a, b)
    page[:, unstriped(offs4)] = np.minimum(a, b)
    w4 = unpack_weight(w4_words, w4_scales, "e2m1")
    y = w4.T @ mxq(page, 0, "e4m3")
    return y + f64(bias2)[:, None]

@@ -1,0 +1,415 @@
+from contextlib import ExitStack
+
+import concourse.mybir as mybir
+
+K, H, N, T, S, T2, PAIRS = 1024, 1024, 512, 2048, 1024, 2048, 512
+FLOPS = 2 * K * H * S + 2 * H * N * T2
+
+F32 = mybir.dt.float32
+BF16 = mybir.dt.bfloat16
+I32 = mybir.dt.int32
+U32 = mybir.dt.uint32
+U16 = mybir.dt.uint16
+U8 = mybir.dt.uint8
+FP8X4 = mybir.dt.float8_e4m3fn_x4
+FP4X4 = mybir.dt.float4_e2m1fn_x4
+ACT = mybir.ActivationFunctionType
+ALU = mybir.AluOpType
+
+P = 128
+PACK = 4
+PASS = P * PACK
+BANK = 512
+QUAD = 32
+PASSES = K // PASS
+SLICES = H // P
+HALVES = S // BANK
+CHUNKS = T2 // BANK
+NTILES = N // P
+
+
+def tile_list_licence_swap_board_kernel(
+    tc, tab_words, tab_scales, offs, w1, bias1, gain, wgs, page0, offs2, offs3, offs4, w4_words, w4_scales, bias2, out
+):
+    nc = tc.nc
+    with ExitStack() as ctx:
+        lists = ctx.enter_context(tc.tile_pool(name="lists", bufs=1))
+        held = ctx.enter_context(tc.tile_pool(name="held", bufs=1))
+        ring = ctx.enter_context(tc.tile_pool(name="ring", bufs=1))
+        psum = ctx.enter_context(tc.psum_pool(name="psum", bufs=8))
+
+        idx = lists.tile([P, S // 16], U16, name="idx")
+        idx2 = lists.tile([P, S // 16], U16, name="idx2")
+        idx3 = lists.tile([P, PAIRS // 16], U16, name="idx3")
+        idx4 = lists.tile([P, PAIRS // 16], U16, name="idx4")
+
+        def half_of(list_tile, half):
+            return list_tile[:, half * (BANK // 16) : (half + 1) * (BANK // 16)]
+
+        tab_w = [ring.tile([P, T], U32, name=f"tab_w{a}", tag="tab", bufs=2) for a in range(PASSES)]
+        tab_s = held.tile([P, T], U8, name="tab_s")
+        b1_first = held.tile([P, 1], F32, name="b1_first")
+        gn_first = held.tile([P, 1], F32, name="gn_first")
+        b1_plain = held.tile([P, PACK - 1], F32, name="b1_plain")
+        gn_plain = held.tile([P, PACK - 1], F32, name="gn_plain")
+        b1_dealt = held.tile([P, PACK], F32, name="b1_dealt")
+        gn_dealt = held.tile([P, PACK], F32, name="gn_dealt")
+        b2 = held.tile([P, NTILES], F32, name="b2")
+        wg_plain = [held.tile([P, BANK], F32, name=f"wg_plain{half}") for half in range(HALVES)]
+        w4w = held.tile([P, PASSES, 2 * N], U8, name="w4w", align_bytes=64)
+        w4s = held.tile([P, PASSES, N], U8, name="w4s", align_bytes=64)
+        wg_dealt = {}
+        w1_raw = {}
+        pages = {}
+
+        def load_table_words(a):
+            nc.sync.dma_start(tab_w[a][:].bitcast(I32), tab_words[a].rearrange("p t i -> p (t i)").bitcast(I32))
+
+        def load_w1(a, c0, c1):
+            if c1 - c0 == P:
+                raw = held.tile([P, PACK, P], F32, name=f"w1_raw_first{a}")
+            else:
+                raw = ring.tile([P, PACK, c1 - c0], F32, name="w1_raw", tag="raw", bufs=4)
+            rows = w1[a * PASS : (a + 1) * PASS, c0:c1]
+            nc.sync.dma_start(raw[:], rows.rearrange("(p j) c -> p j c", j=PACK))
+            w1_raw[a, c0] = raw
+
+        def load_page(s):
+            page = ring.tile([P, T2], F32, name="page", tag="page", bufs=6)
+            if s < PACK:
+                rows = page0[s * P : (s + 1) * P, :]
+            else:
+                rows = page0[PASS:H, :].rearrange("(p t) c -> t p c", t=PACK)[s - PACK]
+            nc.sync.dma_start(page[:], rows)
+            pages[s] = page
+
+        def load_wg_dealt(u):
+            dealt = ring.tile([P, 2, S], F32, name="wg_dealt", tag="tab", bufs=2)
+            rows = wgs.rearrange("(q t) j -> q t j", t=PACK)[:, 2 * u : 2 * u + 2, :]
+            for q in range(P // QUAD):
+                nc.sync.dma_start(dealt[QUAD * q : QUAD * (q + 1), :, :], rows)
+            for e in range(2):
+                wg_dealt[2 * u + e] = dealt[:, e, :]
+
+        nc.vector.memset(tab_s[:].bitcast(I32), 0)
+        with nc.allow_non_contiguous_dma(reason="one value to a partition"):
+            nc.gpsimd.dma_start(gn_first[:], gain[0:P].rearrange("(p s) -> p s", s=1))
+            nc.gpsimd.dma_start(b1_first[:], bias1[0:P].rearrange("(p s) -> p s", s=1))
+        nc.gpsimd.memset(w4s[:].rearrange("p a n -> p (a n)").bitcast(I32), 0)
+
+        nc.sync.dma_start(idx[:], offs)
+        load_table_words(0)
+        for q in range(P // QUAD):
+            nc.sync.dma_start(
+                tab_s[QUAD * q : QUAD * q + 4 * PASSES, :].bitcast(I32), tab_scales[:, 4 * q : 4 * q + 4, :].bitcast(I32)
+            )
+        load_w1(0, 0, P)
+        load_w1(1, 0, P)
+        nc.sync.dma_start(wg_plain[0][:], wgs[:, 0:BANK])
+        load_table_words(1)
+        nc.sync.dma_start(idx2[:], offs2)
+        load_page(0)
+        nc.sync.dma_start(wg_plain[1][:], wgs[:, BANK:S])
+        load_w1(0, P, PASS)
+        load_w1(1, P, PASS)
+        with nc.allow_non_contiguous_dma(reason="one value to a partition"):
+            nc.sync.dma_start(b1_plain[:], bias1[P:PASS].rearrange("(s p) -> p s", p=P))
+            nc.sync.dma_start(gn_plain[:], gain[P:PASS].rearrange("(s p) -> p s", p=P))
+        nc.sync.dma_start(idx3[:], offs3)
+        nc.sync.dma_start(idx4[:], offs4)
+        load_page(1)
+        load_page(2)
+        load_w1(0, PASS, H)
+        load_w1(1, PASS, H)
+        load_page(3)
+        nc.sync.dma_start(w4w[:].bitcast(I32), w4_words.rearrange("a p n -> p a n").bitcast(I32))
+        for q in range(P // QUAD):
+            nc.sync.dma_start(
+                w4s[QUAD * q : QUAD * q + 4, :, :].bitcast(I32),
+                w4_scales[:, 4 * q : 4 * q + 4, :].rearrange("a r n -> r a n").bitcast(I32),
+            )
+        with nc.allow_non_contiguous_dma(reason="one value to a partition"):
+            nc.sync.dma_start(b2[:], bias2.rearrange("(m p) -> p m", p=P))
+        nc.sync.dma_start(b1_dealt[:], bias1[PASS:H].rearrange("(p t) -> p t", t=PACK))
+        nc.sync.dma_start(gn_dealt[:], gain[PASS:H].rearrange("(p t) -> p t", t=PACK))
+        load_wg_dealt(0)
+        load_page(4)
+        load_wg_dealt(1)
+        load_page(5)
+
+        v_w = {}
+        v_s = {}
+
+        def gather_words(a, half):
+            picked = held.tile([P, BANK], U32, name=f"v_w{a}{half}", align_bytes=64)
+            nc.vector.tensor_copy(picked[:], tab_w[a][:].indirect(half_of(idx, half)))
+            v_w[a, half] = picked
+
+        def gather_scales(half):
+            picked = held.tile([P, BANK], U8, name=f"v_s{half}", align_bytes=64)
+            nc.vector.tensor_copy(picked[:], tab_s[:].indirect(half_of(idx, half)))
+            v_s[half] = picked
+
+        w1_woven = {}
+        w1_mx = {}
+
+        def weave_w1(a, c0, c1):
+            width = c1 - c0
+            if width == P:
+                woven = held.tile([P, width * PACK], BF16, name=f"w1_woven_first{a}", align_bytes=64)
+            else:
+                slot = 2 * (c0 // PASS) + a
+                woven = ring.tile([P, width * PACK], BF16, name="w1_woven", tag=f"woven{slot}", bufs=2, align_bytes=64)
+            if c0 < PASS:
+                nc.scalar.copy(
+                    woven[:].rearrange("p (c j) -> p c j", j=PACK), w1_raw[a, c0][:].rearrange("p j c -> p c j")
+                )
+            else:
+                nc.scalar.copy(
+                    woven[:].rearrange("p (t m j) -> p m t j", t=PACK, j=PACK),
+                    w1_raw[a, c0][:].rearrange("p j (m t) -> p m t j", t=PACK),
+                )
+            w1_woven[a, c0] = woven
+
+        def quantize_w1(a, c0, c1):
+            width = c1 - c0
+            codes = held.tile([P, width], U32, name=f"w1_codes{a}_{c0}", align_bytes=64)
+            scales = held.tile([P, width], U8, name=f"w1_scales{a}_{c0}", align_bytes=64)
+            nc.vector.quantize_mx(out=codes[:].bitcast(FP8X4), scales=scales[:], in_=w1_woven[a, c0][:])
+            for s in range(c0 // P, c1 // P):
+                cols = slice(s * P - c0, (s + 1) * P - c0)
+                w1_mx[s, a] = (codes[:, cols], scales[:, cols])
+
+        feats = {}
+        factors = {}
+
+        def features(s, half):
+            b, t = divmod(s, PACK)
+            wg = wg_plain[half][:] if b == 0 else wg_dealt[t][:, half * BANK : (half + 1) * BANK]
+            if s == 0:
+                b1, gn = b1_first[:], gn_first[:]
+            elif b == 0:
+                b1, gn = b1_plain[:, t - 1 : t], gn_plain[:, t - 1 : t]
+            else:
+                b1, gn = b1_dealt[:, t : t + 1], gn_dealt[:, t : t + 1]
+            factor = ring.tile([P, BANK], F32, name="factor", tag="factor", bufs=6)
+            nc.scalar.activation(factor[:], wg, ACT.Copy, scale=gn)
+            acc = psum.tile([P, BANK], F32, name="acc", tag="bank")
+            for a in range(PASSES):
+                codes, scales = w1_mx[s, a]
+                nc.tensor.matmul_mx(
+                    out=acc[:],
+                    lhsT=codes.bitcast(FP8X4),
+                    lhsT_scale=scales,
+                    rhs=v_w[a, half][:].bitcast(FP8X4),
+                    rhs_scale=v_s[half][4 * a : P, :],
+                    start=(a == 0),
+                    stop=(a == PASSES - 1),
+                )
+            feat = ring.tile([P, BANK], F32, name="feat", tag="feat", bufs=6)
+            nc.scalar.activation(feat[:], acc[:], ACT.Tanh, bias=b1)
+            feats[s, half] = feat
+            factors[s, half] = factor
+
+        def put_features(s, half):
+            nc.vector.tensor_tensor(
+                pages[s][:].indirect(half_of(idx2, half)), feats[s, half][:], factors[s, half][:], ALU.mult
+            )
+
+        pair = {}
+
+        def fetch_pairs(s):
+            if s == SLICES - 2:
+                spent = board_woven[0, CHUNKS - 1][:].rearrange("p c t -> p (c t)").bitcast(F32)
+                first, second = spent[:, 0:PAIRS], spent[:, PAIRS : 2 * PAIRS]
+            else:
+                first = ring.tile([P, PAIRS], F32, name="first", tag="first", bufs=2)
+                second = ring.tile([P, PAIRS], F32, name="second", tag="second", bufs=2)
+            nc.vector.tensor_copy(first[:], pages[s][:].indirect(idx3[:]))
+            nc.vector.tensor_copy(second[:], pages[s][:].indirect(idx4[:]))
+            pair[s] = (first, second)
+
+        def order_pairs(s):
+            first, second = pair[s]
+            larger = ring.tile([P, PAIRS], F32, name="larger", tag="larger", bufs=2)
+            smaller = ring.tile([P, PAIRS], F32, name="smaller", tag="smaller", bufs=2)
+            nc.vector.tensor_tensor(larger[:], first[:], second[:], ALU.max)
+            nc.vector.tensor_tensor(smaller[:], first[:], second[:], ALU.min)
+            pair[s] = (larger, smaller)
+
+        def put_larger(s):
+            nc.vector.tensor_copy(pages[s][:].indirect(idx3[:]), pair[s][0][:])
+
+        def put_smaller(s):
+            nc.vector.tensor_copy(pages[s][:].indirect(idx4[:]), pair[s][1][:])
+
+        board_woven = {}
+        board_mx = {}
+        planes = {}
+        sums = {}
+        staged = {}
+
+        def new_woven(b, c):
+            board_woven[b, c] = ring.tile(
+                [P, BANK, PACK], BF16, name="board_woven", tag=f"woven{c}", bufs=2, align_bytes=64
+            )
+
+        def round_and_deal(s):
+            rounded = ring.tile([P, T2], BF16, name="rounded", tag="rounded", bufs=2)
+            nc.scalar.copy(rounded[:], pages[s][:])
+            for u in range(2):
+                if s == 0:
+                    planes[u] = ring.tile([P, PACK, T2 // 2], BF16, name="planes", tag="raw", bufs=4)
+                nc.scalar.dma_start(
+                    planes[u][QUAD * s : QUAD * (s + 1), :, :], rounded[:, u * (T2 // 2) : (u + 1) * (T2 // 2)]
+                )
+
+        def weave_planes(c):
+            new_woven(0, c)
+            u, e = divmod(c, 2)
+            nc.scalar.copy(
+                board_woven[0, c][:], planes[u][:, :, e * BANK : (e + 1) * BANK].rearrange("p t c -> p c t")
+            )
+
+        def weave_page(s, c):
+            t = s - PACK
+            if t == 0:
+                new_woven(1, c)
+            nc.scalar.copy(board_woven[1, c][:, :, t], pages[s][:, c * BANK : (c + 1) * BANK])
+
+        def quantize_board(b, c):
+            codes = held.tile([P, BANK], U32, name="board_codes", tag=f"codes{b}{c}", align_bytes=64)
+            scales = held.tile([P, BANK], U8, name=f"board_scales{b}{c}", align_bytes=64)
+            nc.vector.quantize_mx(
+                out=codes[:].bitcast(FP8X4), scales=scales[:], in_=board_woven[b, c][:].rearrange("p c t -> p (c t)")
+            )
+            board_mx[b, c] = (codes, scales)
+
+        def read_out(b, c, m, start, stop):
+            codes, scales = board_mx[b, c]
+            if start:
+                sums[c, m] = psum.tile([P, BANK], F32, name="acc", tag="bank")
+            nc.tensor.matmul_mx(
+                out=sums[c, m][:],
+                lhsT=w4w[:, b, 2 * P * m : 2 * P * (m + 1)].bitcast(FP4X4),
+                lhsT_scale=w4s[:, b, P * m : P * (m + 1)],
+                rhs=codes[:].bitcast(FP8X4),
+                rhs_scale=scales[:],
+                start=start,
+                stop=stop,
+            )
+
+        kept = [(2, m) for m in range(NTILES)]
+        late = [(3, 2), (3, 3)]
+        parked_in_codes = {(0, 0): 1, (0, 2): 2, (1, 0): 3}
+        parked = {}
+
+        def first_pass(c):
+            staged[c] = ring.tile([P, NTILES, BANK], F32, name="staged", tag="raw", bufs=4)
+            for m in range(NTILES):
+                if (c, m) in late:
+                    continue
+                read_out(0, c, m, True, (c, m) not in kept)
+                if (c, m) in kept:
+                    continue
+                if (c, m) in parked_in_codes:
+                    spot = held.tile(
+                        [P, BANK], F32, name="parked", tag=f"codes1{parked_in_codes[c, m]}", align_bytes=64
+                    )
+                    parked[c, m] = spot[:]
+                else:
+                    parked[c, m] = staged[c][:, m, :]
+                nc.scalar.activation(parked[c, m], sums[c, m][:], ACT.Identity, bias=b2[:, m : m + 1])
+
+        def second_pass(c):
+            for m in range(NTILES):
+                if (c, m) in late:
+                    read_out(0, c, m, True, False)
+                read_out(1, c, m, (c, m) in parked, True)
+
+        def finish(c, m):
+            if (c, m) in parked:
+                nc.vector.tensor_tensor(staged[c][:, m, :], sums[c, m][:], parked[c, m], ALU.add)
+            else:
+                nc.scalar.activation(staged[c][:, m, :], sums[c, m][:], ACT.Identity, bias=b2[:, m : m + 1])
+            nc.sync.dma_start(out[m * P : (m + 1) * P, c * BANK : (c + 1) * BANK], staged[c][:, m, :])
+
+        gather_words(0, 0)
+        gather_scales(0)
+        gather_words(0, 1)
+        for a in range(PASSES):
+            weave_w1(a, 0, P)
+        for a in range(PASSES):
+            quantize_w1(a, 0, P)
+        gather_scales(1)
+        gather_words(1, 0)
+        features(0, 0)
+        gather_words(1, 1)
+        features(0, 1)
+        put_features(0, 0)
+        for a in range(PASSES):
+            weave_w1(a, P, PASS)
+        put_features(0, 1)
+        for a in range(PASSES):
+            quantize_w1(a, P, PASS)
+        for half in range(HALVES):
+            features(1, half)
+        for a in range(PASSES):
+            weave_w1(a, PASS, H)
+
+        for s in range(SLICES):
+            last = s == SLICES - 1
+            if s + 2 < SLICES:
+                if s + 2 == PACK:
+                    for a in range(PASSES):
+                        quantize_w1(a, PASS, H)
+                for half in range(HALVES):
+                    features(s + 2, half)
+            fetch_pairs(s)
+            if not last:
+                put_features(s + 1, 0)
+            order_pairs(s)
+            put_larger(s)
+            if not last:
+                put_features(s + 1, 1)
+            put_smaller(s)
+            if s < PACK:
+                round_and_deal(s)
+            if s == PACK:
+                for c in range(CHUNKS):
+                    weave_planes(c)
+            if s == PACK + 1:
+                for c in range(CHUNKS):
+                    quantize_board(0, c)
+                    first_pass(c)
+            if PACK <= s and not last:
+                for c in range(CHUNKS):
+                    weave_page(s, c)
+            if s + 6 < SLICES:
+                load_page(s + 6)
+        for c in range(CHUNKS):
+            weave_page(SLICES - 1, c)
+        quantize_board(1, 0)
+        second_pass(0)
+        finish(0, 0)
+        finish(0, 1)
+        quantize_board(1, 1)
+        finish(0, 2)
+        finish(0, 3)
+        second_pass(1)
+        quantize_board(1, 2)
+        second_pass(2)
+        finish(1, 0)
+        finish(1, 1)
+        quantize_board(1, 3)
+        finish(2, 0)
+        finish(1, 2)
+        finish(2, 1)
+        finish(1, 3)
+        second_pass(3)
+        finish(2, 2)
+        finish(3, 0)
+        finish(2, 3)
+        finish(3, 1)
+        finish(3, 2)
+        finish(3, 3)

@@ -26,6 +26,7 @@ SLICES = H // P
 HALVES = S // BANK
 CHUNKS = T2 // BANK
 NTILES = N // P
+LANES = (2, 0, 1, 3)
 
 
 def tile_list_licence_swap_board_kernel(
@@ -51,11 +52,10 @@ def tile_list_licence_swap_board_kernel(
         b1_first = held.tile([P, 1], F32, name="b1_first")
         gn_first = held.tile([P, 1], F32, name="gn_first")
         b1_plain = held.tile([P, PACK - 1], F32, name="b1_plain")
-        gn_plain = held.tile([P, PACK - 1], F32, name="gn_plain")
         b1_dealt = held.tile([P, PACK], F32, name="b1_dealt")
-        gn_dealt = held.tile([P, PACK], F32, name="gn_dealt")
+        gains = {}
         b2 = held.tile([P, NTILES], F32, name="b2")
-        wg_plain = [held.tile([P, BANK], F32, name=f"wg_plain{half}") for half in range(HALVES)]
+        wg_plain = held.tile([P, S], F32, name="wg_plain")
         w4w = held.tile([P, PASSES, 2 * N], U8, name="w4w", align_bytes=64)
         w4s = held.tile([P, PASSES, N], U8, name="w4s", align_bytes=64)
         wg_dealt = {}
@@ -67,7 +67,7 @@ def tile_list_licence_swap_board_kernel(
 
         def load_w1(a, c0, c1):
             if c1 - c0 == P:
-                raw = held.tile([P, PACK, P], F32, name=f"w1_raw_first{a}")
+                raw = held.tile([P, PACK, P], F32, name=f"w1_raw{a}_{c0}")
             else:
                 raw = ring.tile([P, PACK, c1 - c0], F32, name="w1_raw", tag="raw", bufs=4)
             rows = w1[a * PASS : (a + 1) * PASS, c0:c1]
@@ -75,13 +75,22 @@ def tile_list_licence_swap_board_kernel(
             w1_raw[a, c0] = raw
 
         def load_page(s):
-            page = ring.tile([P, T2], F32, name="page", tag="page", bufs=6)
+            page = ring.tile([P, T2], F32, name="page", tag="page", bufs=SLICES)
             if s < PACK:
                 rows = page0[s * P : (s + 1) * P, :]
             else:
-                rows = page0[PASS:H, :].rearrange("(p t) c -> t p c", t=PACK)[s - PACK]
+                rows = page0[PASS:H, :].rearrange("(p t) c -> t p c", t=PACK)[LANES[s - PACK]]
             nc.sync.dma_start(page[:], rows)
             pages[s] = page
+            if s > 0:
+                gains[s] = held.tile([P, 1], F32, name=f"gain{s}")
+                if s < PACK:
+                    values = gain[s * P : (s + 1) * P].rearrange("(p o) -> p o", o=1)
+                else:
+                    t = LANES[s - PACK]
+                    values = gain[PASS:H].rearrange("(p t) -> p t", t=PACK)[:, t : t + 1]
+                with nc.allow_non_contiguous_dma(reason="one value to a partition"):
+                    nc.sync.dma_start(gains[s][:], values)
 
         def load_wg_dealt(u):
             dealt = ring.tile([P, 2, S], F32, name="wg_dealt", tag="tab", bufs=2)
@@ -103,25 +112,33 @@ def tile_list_licence_swap_board_kernel(
             nc.sync.dma_start(
                 tab_s[QUAD * q : QUAD * q + 4 * PASSES, :].bitcast(I32), tab_scales[:, 4 * q : 4 * q + 4, :].bitcast(I32)
             )
-        load_w1(0, 0, P)
-        load_w1(1, 0, P)
-        nc.sync.dma_start(wg_plain[0][:], wgs[:, 0:BANK])
         load_table_words(1)
+        load_w1(0, 0, P)
+        nc.sync.dma_start(wg_plain[:, 0:BANK], wgs[:, 0:BANK])
+        load_w1(1, 0, P)
         nc.sync.dma_start(idx2[:], offs2)
         load_page(0)
-        nc.sync.dma_start(wg_plain[1][:], wgs[:, BANK:S])
-        load_w1(0, P, PASS)
-        load_w1(1, P, PASS)
-        with nc.allow_non_contiguous_dma(reason="one value to a partition"):
-            nc.sync.dma_start(b1_plain[:], bias1[P:PASS].rearrange("(s p) -> p s", p=P))
-            nc.sync.dma_start(gn_plain[:], gain[P:PASS].rearrange("(s p) -> p s", p=P))
+        load_w1(0, P, 2 * P)
+        load_w1(1, P, 2 * P)
+        nc.sync.dma_start(wg_plain[:, BANK:S], wgs[:, BANK:S])
         nc.sync.dma_start(idx3[:], offs3)
         nc.sync.dma_start(idx4[:], offs4)
+        with nc.allow_non_contiguous_dma(reason="one value to a partition"):
+            nc.sync.dma_start(b1_plain[:], bias1[P:PASS].rearrange("(s p) -> p s", p=P))
+        load_w1(0, 2 * P, PASS)
+        load_w1(1, 2 * P, PASS)
         load_page(1)
         load_page(2)
         load_w1(0, PASS, H)
         load_w1(1, PASS, H)
         load_page(3)
+        nc.sync.dma_start(b1_dealt[:], bias1[PASS:H].rearrange("(p t) -> p t", t=PACK))
+        load_wg_dealt(1)
+        load_page(4)
+        load_wg_dealt(0)
+        load_page(5)
+        load_page(6)
+        load_page(7)
         nc.sync.dma_start(w4w[:].bitcast(I32), w4_words.rearrange("a p n -> p a n").bitcast(I32))
         for q in range(P // QUAD):
             nc.sync.dma_start(
@@ -130,73 +147,59 @@ def tile_list_licence_swap_board_kernel(
             )
         with nc.allow_non_contiguous_dma(reason="one value to a partition"):
             nc.sync.dma_start(b2[:], bias2.rearrange("(m p) -> p m", p=P))
-        nc.sync.dma_start(b1_dealt[:], bias1[PASS:H].rearrange("(p t) -> p t", t=PACK))
-        nc.sync.dma_start(gn_dealt[:], gain[PASS:H].rearrange("(p t) -> p t", t=PACK))
-        load_wg_dealt(0)
-        load_page(4)
-        load_wg_dealt(1)
-        load_page(5)
 
         v_w = {}
         v_s = {}
 
         def gather_words(a, half):
-            picked = held.tile([P, BANK], U32, name=f"v_w{a}{half}", align_bytes=64)
+            tag = "woven_first1" if (a, half) == (1, 1) else f"v_w{a}{half}"
+            picked = ring.tile([P, BANK], U32, name="v_w", tag=tag, bufs=1, align_bytes=64)
             nc.vector.tensor_copy(picked[:], tab_w[a][:].indirect(half_of(idx, half)))
             v_w[a, half] = picked
 
         def gather_scales(half):
-            picked = held.tile([P, BANK], U8, name=f"v_s{half}", align_bytes=64)
+            picked = ring.tile([P, BANK], U8, name="v_s", tag=("v_s0", "woven_first0")[half], bufs=1, align_bytes=64)
             nc.vector.tensor_copy(picked[:], tab_s[:].indirect(half_of(idx, half)))
             v_s[half] = picked
 
         w1_woven = {}
         w1_mx = {}
 
-        def weave_w1(a, c0, c1):
+        def weave_w1(passes, c0, c1, tag):
             width = c1 - c0
-            if width == P:
-                woven = held.tile([P, width * PACK], BF16, name=f"w1_woven_first{a}", align_bytes=64)
-            else:
-                slot = 2 * (c0 // PASS) + a
-                woven = ring.tile([P, width * PACK], BF16, name="w1_woven", tag=f"woven{slot}", bufs=2, align_bytes=64)
-            if c0 < PASS:
-                nc.scalar.copy(
-                    woven[:].rearrange("p (c j) -> p c j", j=PACK), w1_raw[a, c0][:].rearrange("p j c -> p c j")
-                )
-            else:
-                nc.scalar.copy(
-                    woven[:].rearrange("p (t m j) -> p m t j", t=PACK, j=PACK),
-                    w1_raw[a, c0][:].rearrange("p j (m t) -> p m t j", t=PACK),
-                )
-            w1_woven[a, c0] = woven
+            woven = ring.tile(
+                [P, len(passes), width * PACK], BF16, name="w1_woven", tag=tag, bufs=1, align_bytes=64
+            )
+            for e, a in enumerate(passes):
+                if c0 < PASS:
+                    nc.scalar.copy(
+                        woven[:, e, :].rearrange("p (c j) -> p c j", j=PACK),
+                        w1_raw[a, c0][:].rearrange("p j c -> p c j"),
+                    )
+                else:
+                    nc.scalar.copy(
+                        woven[:, e, :].rearrange("p (t m j) -> p m t j", t=PACK, j=PACK),
+                        w1_raw[a, c0][:].rearrange("p j (m t) -> p m t j", t=PACK),
+                    )
+            w1_woven[passes, c0] = woven[:].rearrange("p a c -> p (a c)")
 
-        def quantize_w1(a, c0, c1):
+        def quantize_w1(passes, c0, c1):
             width = c1 - c0
-            codes = held.tile([P, width], U32, name=f"w1_codes{a}_{c0}", align_bytes=64)
-            scales = held.tile([P, width], U8, name=f"w1_scales{a}_{c0}", align_bytes=64)
-            nc.vector.quantize_mx(out=codes[:].bitcast(FP8X4), scales=scales[:], in_=w1_woven[a, c0][:])
-            for s in range(c0 // P, c1 // P):
-                cols = slice(s * P - c0, (s + 1) * P - c0)
-                w1_mx[s, a] = (codes[:, cols], scales[:, cols])
+            codes = held.tile([P, len(passes) * width], U32, name=f"w1_codes{passes[0]}_{c0}", align_bytes=64)
+            scales = held.tile([P, len(passes) * width], U8, name=f"w1_scales{passes[0]}_{c0}", align_bytes=64)
+            nc.vector.quantize_mx(out=codes[:].bitcast(FP8X4), scales=scales[:], in_=w1_woven[passes, c0])
+            for e, a in enumerate(passes):
+                for s in range(c0 // P, c1 // P):
+                    cols = slice(e * width + s * P - c0, e * width + (s + 1) * P - c0)
+                    w1_mx[s, a] = (codes[:, cols], scales[:, cols])
 
+        squashed = {}
         feats = {}
-        factors = {}
 
-        def features(s, half):
-            b, t = divmod(s, PACK)
-            wg = wg_plain[half][:] if b == 0 else wg_dealt[t][:, half * BANK : (half + 1) * BANK]
-            if s == 0:
-                b1, gn = b1_first[:], gn_first[:]
-            elif b == 0:
-                b1, gn = b1_plain[:, t - 1 : t], gn_plain[:, t - 1 : t]
-            else:
-                b1, gn = b1_dealt[:, t : t + 1], gn_dealt[:, t : t + 1]
-            factor = ring.tile([P, BANK], F32, name="factor", tag="factor", bufs=6)
-            nc.scalar.activation(factor[:], wg, ACT.Copy, scale=gn)
+        def squash(s, half, b1):
             acc = psum.tile([P, BANK], F32, name="acc", tag="bank")
             for a in range(PASSES):
-                codes, scales = w1_mx[s, a]
+                codes, scales = w1_mx[s if s < PACK else PACK + LANES[s - PACK], a]
                 nc.tensor.matmul_mx(
                     out=acc[:],
                     lhsT=codes.bitcast(FP8X4),
@@ -206,42 +209,65 @@ def tile_list_licence_swap_board_kernel(
                     start=(a == 0),
                     stop=(a == PASSES - 1),
                 )
-            feat = ring.tile([P, BANK], F32, name="feat", tag="feat", bufs=6)
-            nc.scalar.activation(feat[:], acc[:], ACT.Tanh, bias=b1)
-            feats[s, half] = feat
-            factors[s, half] = factor
+            nc.scalar.activation(squashed[s][:, half * BANK : (half + 1) * BANK], acc[:], ACT.Tanh, bias=b1)
 
-        def put_features(s, half):
+        def new_squashed(s):
+            squashed[s] = ring.tile([P, S], F32, name="squashed", tag="squashed", bufs=3)
+
+        def first_features(half):
+            cols = slice(half * BANK, (half + 1) * BANK)
+            if half == 0:
+                new_squashed(0)
+                feats[0] = ring.tile([P, S], F32, name="feat", tag="feat", bufs=2)
+            nc.scalar.activation(feats[0][:, cols], wg_plain[:, cols], ACT.Copy, scale=gn_first[:])
+            squash(0, half, b1_first[:])
+
+        def put_first_features(half):
+            cols = slice(half * BANK, (half + 1) * BANK)
             nc.vector.tensor_tensor(
-                pages[s][:].indirect(half_of(idx2, half)), feats[s, half][:], factors[s, half][:], ALU.mult
+                pages[0][:].indirect(half_of(idx2, half)), squashed[0][:, cols], feats[0][:, cols], ALU.mult
             )
+
+        def features(s):
+            if s < PACK:
+                b1 = b1_plain[:, s - 1 : s]
+            else:
+                b1 = b1_dealt[:, LANES[s - PACK] : LANES[s - PACK] + 1]
+            new_squashed(s)
+            for half in range(HALVES):
+                squash(s, half, b1)
+            feats[s] = ring.tile([P, S], F32, name="feat", tag="feat", bufs=2)
+            nc.scalar.activation(feats[s][:], squashed[s][:], ACT.Copy, scale=gains[s][:])
+
+        def put_features(s):
+            wg = wg_plain[:] if s < PACK else wg_dealt[LANES[s - PACK]]
+            nc.vector.tensor_tensor(pages[s][:].indirect(idx2[:]), feats[s][:], wg, ALU.mult)
 
         pair = {}
 
-        def fetch_pairs(s):
-            if s == SLICES - 2:
-                spent = board_woven[0, CHUNKS - 1][:].rearrange("p c t -> p (c t)").bitcast(F32)
-                first, second = spent[:, 0:PAIRS], spent[:, PAIRS : 2 * PAIRS]
-            else:
-                first = ring.tile([P, PAIRS], F32, name="first", tag="first", bufs=2)
-                second = ring.tile([P, PAIRS], F32, name="second", tag="second", bufs=2)
-            nc.vector.tensor_copy(first[:], pages[s][:].indirect(idx3[:]))
-            nc.vector.tensor_copy(second[:], pages[s][:].indirect(idx4[:]))
+        def fetch_pairs(s, first=None, second=None):
+            if first is None:
+                first = ring.tile([P, PAIRS], F32, name="first", tag="first", bufs=2)[:]
+            if second is None:
+                second = ring.tile([P, PAIRS], F32, name="second", tag="second", bufs=2)[:]
+            nc.vector.tensor_copy(first, pages[s][:].indirect(idx3[:]))
+            nc.vector.tensor_copy(second, pages[s][:].indirect(idx4[:]))
             pair[s] = (first, second)
 
         def order_pairs(s):
             first, second = pair[s]
-            larger = ring.tile([P, PAIRS], F32, name="larger", tag="larger", bufs=2)
-            smaller = ring.tile([P, PAIRS], F32, name="smaller", tag="smaller", bufs=2)
-            nc.vector.tensor_tensor(larger[:], first[:], second[:], ALU.max)
-            nc.vector.tensor_tensor(smaller[:], first[:], second[:], ALU.min)
+            if s + 1 == SLICES:
+                new_squashed(SLICES)
+            larger, smaller = squashed[s + 1][:, 0:PAIRS], squashed[s + 1][:, PAIRS : 2 * PAIRS]
+            nc.vector.tensor_tensor(larger, first, second, ALU.max)
+            nc.vector.tensor_tensor(smaller, first, second, ALU.min)
             pair[s] = (larger, smaller)
 
         def put_larger(s):
-            nc.vector.tensor_copy(pages[s][:].indirect(idx3[:]), pair[s][0][:])
+            nc.vector.tensor_copy(pages[s][:].indirect(idx3[:]), pair[s][0])
 
-        def put_smaller(s):
-            nc.vector.tensor_copy(pages[s][:].indirect(idx4[:]), pair[s][1][:])
+        def put_smaller(s, ordered):
+            nc.vector.tensor_copy(pages[s][:].indirect(idx4[:]), ordered[1])
 
         board_woven = {}
         board_mx = {}
@@ -251,34 +277,30 @@ def tile_list_licence_swap_board_kernel(
 
         def new_woven(b, c):
             board_woven[b, c] = ring.tile(
-                [P, BANK, PACK], BF16, name="board_woven", tag=f"woven{c}", bufs=2, align_bytes=64
+                [P, BANK, PACK], BF16, name="board_woven", tag=f"{('woven', 'planes')[b]}{c}", bufs=1, align_bytes=64
             )
 
         def round_and_deal(s):
-            rounded = ring.tile([P, T2], BF16, name="rounded", tag="rounded", bufs=2)
+            rounded = ring.tile([P, T2], BF16, name="rounded", tag="rounded", bufs=1)
             nc.scalar.copy(rounded[:], pages[s][:])
-            for u in range(2):
+            for c in range(CHUNKS):
                 if s == 0:
-                    planes[u] = ring.tile([P, PACK, T2 // 2], BF16, name="planes", tag="raw", bufs=4)
-                nc.scalar.dma_start(
-                    planes[u][QUAD * s : QUAD * (s + 1), :, :], rounded[:, u * (T2 // 2) : (u + 1) * (T2 // 2)]
-                )
+                    planes[c] = ring.tile([P, PACK, BANK], BF16, name="planes", tag=f"planes{c}", bufs=1, align_bytes=64)
+                nc.scalar.dma_start(planes[c][QUAD * s : QUAD * (s + 1), :, :], rounded[:, c * BANK : (c + 1) * BANK])
 
         def weave_planes(c):
             new_woven(0, c)
-            u, e = divmod(c, 2)
-            nc.scalar.copy(
-                board_woven[0, c][:], planes[u][:, :, e * BANK : (e + 1) * BANK].rearrange("p t c -> p c t")
-            )
+            nc.scalar.copy(board_woven[0, c][:], planes[c][:].rearrange("p t c -> p c t"))
 
         def weave_page(s, c):
-            t = s - PACK
-            if t == 0:
+            if s == PACK:
                 new_woven(1, c)
-            nc.scalar.copy(board_woven[1, c][:, :, t], pages[s][:, c * BANK : (c + 1) * BANK])
+            copy = nc.vector.tensor_copy if s == SLICES - 1 else nc.scalar.copy
+            copy(board_woven[1, c][:, :, LANES[s - PACK]], pages[s][:, c * BANK : (c + 1) * BANK])
 
         def quantize_board(b, c):
-            codes = held.tile([P, BANK], U32, name="board_codes", tag=f"codes{b}{c}", align_bytes=64)
+            tag = f"codes1{c}" if b == 1 else ("first_spent", "second_spent", "woven0", "woven1")[c]
+            codes = ring.tile([P, BANK], U32, name="board_codes", tag=tag, bufs=1, align_bytes=64)
             scales = held.tile([P, BANK], U8, name=f"board_scales{b}{c}", align_bytes=64)
             nc.vector.quantize_mx(
                 out=codes[:].bitcast(FP8X4), scales=scales[:], in_=board_woven[b, c][:].rearrange("p c t -> p (c t)")
@@ -299,117 +321,82 @@ def tile_list_licence_swap_board_kernel(
                 stop=stop,
             )
 
-        kept = [(2, m) for m in range(NTILES)]
-        late = [(3, 2), (3, 3)]
-        parked_in_codes = {(0, 0): 1, (0, 2): 2, (1, 0): 3}
-        parked = {}
-
-        def first_pass(c):
-            staged[c] = ring.tile([P, NTILES, BANK], F32, name="staged", tag="raw", bufs=4)
-            for m in range(NTILES):
-                if (c, m) in late:
-                    continue
-                read_out(0, c, m, True, (c, m) not in kept)
-                if (c, m) in kept:
-                    continue
-                if (c, m) in parked_in_codes:
-                    spot = held.tile(
-                        [P, BANK], F32, name="parked", tag=f"codes1{parked_in_codes[c, m]}", align_bytes=64
-                    )
-                    parked[c, m] = spot[:]
-                else:
-                    parked[c, m] = staged[c][:, m, :]
-                nc.scalar.activation(parked[c, m], sums[c, m][:], ACT.Identity, bias=b2[:, m : m + 1])
-
-        def second_pass(c):
-            for m in range(NTILES):
-                if (c, m) in late:
-                    read_out(0, c, m, True, False)
-                read_out(1, c, m, (c, m) in parked, True)
-
         def finish(c, m):
-            if (c, m) in parked:
-                nc.vector.tensor_tensor(staged[c][:, m, :], sums[c, m][:], parked[c, m], ALU.add)
+            if m == 0:
+                staged[c] = ring.tile([P, NTILES, BANK], F32, name="staged", tag="raw", bufs=4)
+            if m == 0 or (c == CHUNKS - 1 and m < NTILES - 1):
+                nc.vector.tensor_scalar_add(staged[c][:, m, :], sums[c, m][:], b2[:, m : m + 1])
             else:
                 nc.scalar.activation(staged[c][:, m, :], sums[c, m][:], ACT.Identity, bias=b2[:, m : m + 1])
             nc.sync.dma_start(out[m * P : (m + 1) * P, c * BANK : (c + 1) * BANK], staged[c][:, m, :])
 
+        both = (0, 1)
+        early = 2
         gather_words(0, 0)
         gather_scales(0)
         gather_words(0, 1)
-        for a in range(PASSES):
-            weave_w1(a, 0, P)
-        for a in range(PASSES):
-            quantize_w1(a, 0, P)
-        gather_scales(1)
         gather_words(1, 0)
-        features(0, 0)
+        for a in both:
+            weave_w1((a,), 0, P, f"woven_first{a}")
+        for a in both:
+            quantize_w1((a,), 0, P)
+        first_features(0)
+        gather_scales(1)
         gather_words(1, 1)
-        features(0, 1)
-        put_features(0, 0)
-        for a in range(PASSES):
-            weave_w1(a, P, PASS)
-        put_features(0, 1)
-        for a in range(PASSES):
-            quantize_w1(a, P, PASS)
-        for half in range(HALVES):
-            features(1, half)
-        for a in range(PASSES):
-            weave_w1(a, PASS, H)
+        put_first_features(0)
+        weave_w1(both, P, 2 * P, "woven1")
+        first_features(1)
+        quantize_w1(both, P, 2 * P)
+        put_first_features(1)
+        weave_w1(both, 2 * P, PASS, "woven0")
+        features(1)
+        quantize_w1(both, 2 * P, PASS)
+        fetch_pairs(
+            0, w1_woven[both, P].bitcast(F32)[:, 0:PAIRS], w1_woven[both, 2 * P].bitcast(F32)[:, 0:PAIRS]
+        )
+        for a in both:
+            weave_w1((a,), PASS, H, f"woven{2 + a}")
 
         for s in range(SLICES):
             last = s == SLICES - 1
             if s + 2 < SLICES:
-                if s + 2 == PACK:
-                    for a in range(PASSES):
-                        quantize_w1(a, PASS, H)
-                for half in range(HALVES):
-                    features(s + 2, half)
-            fetch_pairs(s)
+                features(s + 2)
             if not last:
-                put_features(s + 1, 0)
+                put_features(s + 1)
             order_pairs(s)
             put_larger(s)
-            if not last:
-                put_features(s + 1, 1)
-            put_smaller(s)
+            if s == 1:
+                for a in both:
+                    quantize_w1((a,), PASS, H)
+                fetch_pairs(s + 1, w1_woven[(1,), PASS].bitcast(F32)[:, 0:PAIRS])
+            elif s == PACK + 1:
+                for c in range(CHUNKS):
+                    quantize_board(0, c)
+                    if c < early:
+                        for m in range(NTILES):
+                            read_out(0, c, m, True, False)
+                spent = board_woven[0, CHUNKS - 1][:].rearrange("p c t -> p (c t)").bitcast(F32)
+                fetch_pairs(s + 1, None, spent[:, 0:PAIRS])
+            elif s == PACK:
+                first = ring.tile([P, PAIRS], F32, name="first", tag="first_spent", bufs=1, align_bytes=64)
+                second = ring.tile([P, PAIRS], F32, name="second", tag="second_spent", bufs=1, align_bytes=64)
+                fetch_pairs(s + 1, first[:], second[:])
+            elif not last:
+                fetch_pairs(s + 1)
+            put_smaller(s, pair[s])
             if s < PACK:
                 round_and_deal(s)
             if s == PACK:
                 for c in range(CHUNKS):
                     weave_planes(c)
-            if s == PACK + 1:
-                for c in range(CHUNKS):
-                    quantize_board(0, c)
-                    first_pass(c)
             if PACK <= s and not last:
                 for c in range(CHUNKS):
                     weave_page(s, c)
-            if s + 6 < SLICES:
-                load_page(s + 6)
         for c in range(CHUNKS):
             weave_page(SLICES - 1, c)
-        quantize_board(1, 0)
-        second_pass(0)
-        finish(0, 0)
-        finish(0, 1)
-        quantize_board(1, 1)
-        finish(0, 2)
-        finish(0, 3)
-        second_pass(1)
-        quantize_board(1, 2)
-        second_pass(2)
-        finish(1, 0)
-        finish(1, 1)
-        quantize_board(1, 3)
-        finish(2, 0)
-        finish(1, 2)
-        finish(2, 1)
-        finish(1, 3)
-        second_pass(3)
-        finish(2, 2)
-        finish(3, 0)
-        finish(2, 3)
-        finish(3, 1)
-        finish(3, 2)
-        finish(3, 3)
+            quantize_board(1, c)
+            for m in range(NTILES):
+                if c >= early:
+                    read_out(0, c, m, True, False)
+                read_out(1, c, m, False, True)
+                finish(c, m)

@@ -75,7 +75,7 @@ def tile_list_licence_swap_board_kernel(
             w1_raw[a, c0] = raw
 
         def load_page(s):
-            page = ring.tile([P, T2], F32, name="page", tag="page", bufs=SLICES)
+            page = ring.tile([P, T2], F32, name="page", tag=f"page{s}", bufs=1)
             if s < PACK:
                 rows = page0[s * P : (s + 1) * P, :]
             else:
@@ -94,12 +94,16 @@ def tile_list_licence_swap_board_kernel(
 
         def load_wg_dealt(u):
             dealt = ring.tile([P, 2, S], F32, name="wg_dealt", tag="tab", bufs=2)
-            rows = wgs.rearrange("(q t) j -> q t j", t=PACK)[:, 2 * u : 2 * u + 2, :]
+            rows = wgs.rearrange("(q t) j -> q t j", t=PACK)[:, u:PACK:2, :]
             for q in range(P // QUAD):
                 nc.sync.dma_start(dealt[QUAD * q : QUAD * (q + 1), :, :], rows)
             for e in range(2):
-                wg_dealt[2 * u + e] = dealt[:, e, :]
+                wg_dealt[u + 2 * e] = dealt[:, e, :]
 
+        warm_in = held.tile([P, 1], F32, name="warm_in")
+        warm_out = held.tile([P, 1], F32, name="warm_out")
+        nc.gpsimd.memset(warm_in[:], 0.0)
+        nc.scalar.activation(warm_out[:], warm_in[:], ACT.Tanh)
         nc.vector.memset(tab_s[:].bitcast(I32), 0)
         with nc.allow_non_contiguous_dma(reason="one value to a partition"):
             nc.gpsimd.dma_start(gn_first[:], gain[0:P].rearrange("(p s) -> p s", s=1))
@@ -113,8 +117,8 @@ def tile_list_licence_swap_board_kernel(
                 tab_s[QUAD * q : QUAD * q + 4 * PASSES, :].bitcast(I32), tab_scales[:, 4 * q : 4 * q + 4, :].bitcast(I32)
             )
         load_table_words(1)
-        load_w1(0, 0, P)
         nc.sync.dma_start(wg_plain[:, 0:BANK], wgs[:, 0:BANK])
+        load_w1(0, 0, P)
         load_w1(1, 0, P)
         nc.sync.dma_start(idx2[:], offs2)
         load_page(0)
@@ -133,10 +137,10 @@ def tile_list_licence_swap_board_kernel(
         load_w1(1, PASS, H)
         load_page(3)
         nc.sync.dma_start(b1_dealt[:], bias1[PASS:H].rearrange("(p t) -> p t", t=PACK))
-        load_wg_dealt(1)
-        load_page(4)
         load_wg_dealt(0)
+        load_page(4)
         load_page(5)
+        load_wg_dealt(1)
         load_page(6)
         load_page(7)
         nc.sync.dma_start(w4w[:].bitcast(I32), w4_words.rearrange("a p n -> p a n").bitcast(I32))
@@ -212,7 +216,10 @@ def tile_list_licence_swap_board_kernel(
             nc.scalar.activation(squashed[s][:, half * BANK : (half + 1) * BANK], acc[:], ACT.Tanh, bias=b1)
 
         def new_squashed(s):
-            squashed[s] = ring.tile([P, S], F32, name="squashed", tag="squashed", bufs=3)
+            if s == SLICES:
+                squashed[s] = ring.tile([P, S], F32, name="squashed", tag=f"page{PACK + 1}", bufs=1)
+            else:
+                squashed[s] = ring.tile([P, S], F32, name="squashed", tag="squashed", bufs=3)
 
         def first_features(half):
             cols = slice(half * BANK, (half + 1) * BANK)

from contextlib import ExitStack

import concourse.mybir as mybir

K, H, N, T, S, T2, PAIRS = 1024, 1024, 512, 2048, 1024, 2048, 512
FLOPS = 2 * K * H * S + 2 * H * N * T2

F32 = mybir.dt.float32
BF16 = mybir.dt.bfloat16
I32 = mybir.dt.int32
U32 = mybir.dt.uint32
U16 = mybir.dt.uint16
U8 = mybir.dt.uint8
FP8X4 = mybir.dt.float8_e4m3fn_x4
FP4X4 = mybir.dt.float4_e2m1fn_x4
ACT = mybir.ActivationFunctionType
ALU = mybir.AluOpType

P = 128
PACK = 4
PASS = P * PACK
BANK = 512
QUAD = 32
PASSES = K // PASS
SLICES = H // P
HALVES = S // BANK
CHUNKS = T2 // BANK
NTILES = N // P
LANES = (2, 0, 1, 3)


def tile_list_licence_swap_board_kernel(
    tc, tab_words, tab_scales, offs, w1, bias1, gain, wgs, page0, offs2, offs3, offs4, w4_words, w4_scales, bias2, out
):
    nc = tc.nc
    with ExitStack() as ctx:
        lists = ctx.enter_context(tc.tile_pool(name="lists", bufs=1))
        held = ctx.enter_context(tc.tile_pool(name="held", bufs=1))
        ring = ctx.enter_context(tc.tile_pool(name="ring", bufs=1))
        psum = ctx.enter_context(tc.psum_pool(name="psum", bufs=8))

        idx = lists.tile([P, S // 16], U16, name="idx")
        idx2 = lists.tile([P, S // 16], U16, name="idx2")
        idx3 = lists.tile([P, PAIRS // 16], U16, name="idx3")
        idx4 = lists.tile([P, PAIRS // 16], U16, name="idx4")

        def half_of(list_tile, half):
            return list_tile[:, half * (BANK // 16) : (half + 1) * (BANK // 16)]

        tab_w = [ring.tile([P, T], U32, name=f"tab_w{a}", tag="tab", bufs=2) for a in range(PASSES)]
        tab_s = held.tile([P, T], U8, name="tab_s")
        b1_first = held.tile([P, 1], F32, name="b1_first")
        gn_first = held.tile([P, 1], F32, name="gn_first")
        b1_plain = held.tile([P, PACK - 1], F32, name="b1_plain")
        b1_dealt = held.tile([P, PACK], F32, name="b1_dealt")
        gains = {}
        b2 = held.tile([P, NTILES], F32, name="b2")
        wg_plain = held.tile([P, S], F32, name="wg_plain")
        w4w = held.tile([P, PASSES, 2 * N], U8, name="w4w", align_bytes=64)
        w4s = held.tile([P, PASSES, N], U8, name="w4s", align_bytes=64)
        wg_dealt = {}
        w1_raw = {}
        pages = {}

        def load_table_words(a):
            nc.sync.dma_start(tab_w[a][:].bitcast(I32), tab_words[a].rearrange("p t i -> p (t i)").bitcast(I32))

        def load_w1(a, c0, c1):
            if c1 - c0 == P:
                raw = held.tile([P, PACK, P], F32, name=f"w1_raw{a}_{c0}")
            else:
                raw = ring.tile([P, PACK, c1 - c0], F32, name="w1_raw", tag="raw", bufs=4)
            rows = w1[a * PASS : (a + 1) * PASS, c0:c1]
            nc.sync.dma_start(raw[:], rows.rearrange("(p j) c -> p j c", j=PACK))
            w1_raw[a, c0] = raw

        def load_page(s):
            page = ring.tile([P, T2], F32, name="page", tag=f"page{s}", bufs=1)
            if s < PACK:
                rows = page0[s * P : (s + 1) * P, :]
            else:
                rows = page0[PASS:H, :].rearrange("(p t) c -> t p c", t=PACK)[LANES[s - PACK]]
            nc.sync.dma_start(page[:], rows)
            pages[s] = page
            if s > 0:
                gains[s] = held.tile([P, 1], F32, name=f"gain{s}")
                if s < PACK:
                    values = gain[s * P : (s + 1) * P].rearrange("(p o) -> p o", o=1)
                else:
                    t = LANES[s - PACK]
                    values = gain[PASS:H].rearrange("(p t) -> p t", t=PACK)[:, t : t + 1]
                with nc.allow_non_contiguous_dma(reason="one value to a partition"):
                    nc.sync.dma_start(gains[s][:], values)

        def load_wg_dealt(u):
            dealt = ring.tile([P, 2, S], F32, name="wg_dealt", tag="tab", bufs=2)
            rows = wgs.rearrange("(q t) j -> q t j", t=PACK)[:, u:PACK:2, :]
            for q in range(P // QUAD):
                nc.sync.dma_start(dealt[QUAD * q : QUAD * (q + 1), :, :], rows)
            for e in range(2):
                wg_dealt[u + 2 * e] = dealt[:, e, :]

        warm_in = held.tile([P, 1], F32, name="warm_in")
        warm_out = held.tile([P, 1], F32, name="warm_out")
        nc.gpsimd.memset(warm_in[:], 0.0)
        nc.scalar.activation(warm_out[:], warm_in[:], ACT.Tanh)
        nc.vector.memset(tab_s[:].bitcast(I32), 0)
        with nc.allow_non_contiguous_dma(reason="one value to a partition"):
            nc.gpsimd.dma_start(gn_first[:], gain[0:P].rearrange("(p s) -> p s", s=1))
            nc.gpsimd.dma_start(b1_first[:], bias1[0:P].rearrange("(p s) -> p s", s=1))
        nc.gpsimd.memset(w4s[:].rearrange("p a n -> p (a n)").bitcast(I32), 0)

        nc.sync.dma_start(idx[:], offs)
        load_table_words(0)
        for q in range(P // QUAD):
            nc.sync.dma_start(
                tab_s[QUAD * q : QUAD * q + 4 * PASSES, :].bitcast(I32), tab_scales[:, 4 * q : 4 * q + 4, :].bitcast(I32)
            )
        load_table_words(1)
        nc.sync.dma_start(wg_plain[:, 0:BANK], wgs[:, 0:BANK])
        load_w1(0, 0, P)
        load_w1(1, 0, P)
        nc.sync.dma_start(idx2[:], offs2)
        load_page(0)
        load_w1(0, P, 2 * P)
        load_w1(1, P, 2 * P)
        nc.sync.dma_start(wg_plain[:, BANK:S], wgs[:, BANK:S])
        nc.sync.dma_start(idx3[:], offs3)
        nc.sync.dma_start(idx4[:], offs4)
        with nc.allow_non_contiguous_dma(reason="one value to a partition"):
            nc.sync.dma_start(b1_plain[:], bias1[P:PASS].rearrange("(s p) -> p s", p=P))
        load_w1(0, 2 * P, PASS)
        load_w1(1, 2 * P, PASS)
        load_page(1)
        load_page(2)
        load_w1(0, PASS, H)
        load_w1(1, PASS, H)
        load_page(3)
        nc.sync.dma_start(b1_dealt[:], bias1[PASS:H].rearrange("(p t) -> p t", t=PACK))
        load_wg_dealt(0)
        load_page(4)
        load_page(5)
        load_wg_dealt(1)
        load_page(6)
        load_page(7)
        nc.sync.dma_start(w4w[:].bitcast(I32), w4_words.rearrange("a p n -> p a n").bitcast(I32))
        for q in range(P // QUAD):
            nc.sync.dma_start(
                w4s[QUAD * q : QUAD * q + 4, :, :].bitcast(I32),
                w4_scales[:, 4 * q : 4 * q + 4, :].rearrange("a r n -> r a n").bitcast(I32),
            )
        with nc.allow_non_contiguous_dma(reason="one value to a partition"):
            nc.sync.dma_start(b2[:], bias2.rearrange("(m p) -> p m", p=P))

        v_w = {}
        v_s = {}

        def gather_words(a, half):
            tag = "woven_first1" if (a, half) == (1, 1) else f"v_w{a}{half}"
            picked = ring.tile([P, BANK], U32, name="v_w", tag=tag, bufs=1, align_bytes=64)
            nc.vector.tensor_copy(picked[:], tab_w[a][:].indirect(half_of(idx, half)))
            v_w[a, half] = picked

        def gather_scales(half):
            picked = ring.tile([P, BANK], U8, name="v_s", tag=("v_s0", "woven_first0")[half], bufs=1, align_bytes=64)
            nc.vector.tensor_copy(picked[:], tab_s[:].indirect(half_of(idx, half)))
            v_s[half] = picked

        w1_woven = {}
        w1_mx = {}

        def weave_w1(passes, c0, c1, tag):
            width = c1 - c0
            woven = ring.tile(
                [P, len(passes), width * PACK], BF16, name="w1_woven", tag=tag, bufs=1, align_bytes=64
            )
            for e, a in enumerate(passes):
                if c0 < PASS:
                    nc.scalar.copy(
                        woven[:, e, :].rearrange("p (c j) -> p c j", j=PACK),
                        w1_raw[a, c0][:].rearrange("p j c -> p c j"),
                    )
                else:
                    nc.scalar.copy(
                        woven[:, e, :].rearrange("p (t m j) -> p m t j", t=PACK, j=PACK),
                        w1_raw[a, c0][:].rearrange("p j (m t) -> p m t j", t=PACK),
                    )
            w1_woven[passes, c0] = woven[:].rearrange("p a c -> p (a c)")

        def quantize_w1(passes, c0, c1):
            width = c1 - c0
            codes = held.tile([P, len(passes) * width], U32, name=f"w1_codes{passes[0]}_{c0}", align_bytes=64)
            scales = held.tile([P, len(passes) * width], U8, name=f"w1_scales{passes[0]}_{c0}", align_bytes=64)
            nc.vector.quantize_mx(out=codes[:].bitcast(FP8X4), scales=scales[:], in_=w1_woven[passes, c0])
            for e, a in enumerate(passes):
                for s in range(c0 // P, c1 // P):
                    cols = slice(e * width + s * P - c0, e * width + (s + 1) * P - c0)
                    w1_mx[s, a] = (codes[:, cols], scales[:, cols])

        squashed = {}
        feats = {}

        def squash(s, half, b1):
            acc = psum.tile([P, BANK], F32, name="acc", tag="bank")
            for a in range(PASSES):
                codes, scales = w1_mx[s if s < PACK else PACK + LANES[s - PACK], a]
                nc.tensor.matmul_mx(
                    out=acc[:],
                    lhsT=codes.bitcast(FP8X4),
                    lhsT_scale=scales,
                    rhs=v_w[a, half][:].bitcast(FP8X4),
                    rhs_scale=v_s[half][4 * a : P, :],
                    start=(a == 0),
                    stop=(a == PASSES - 1),
                )
            nc.scalar.activation(squashed[s][:, half * BANK : (half + 1) * BANK], acc[:], ACT.Tanh, bias=b1)

        def new_squashed(s):
            if s == SLICES:
                squashed[s] = ring.tile([P, S], F32, name="squashed", tag=f"page{PACK + 1}", bufs=1)
            else:
                squashed[s] = ring.tile([P, S], F32, name="squashed", tag="squashed", bufs=3)

        def first_features(half):
            cols = slice(half * BANK, (half + 1) * BANK)
            if half == 0:
                new_squashed(0)
                feats[0] = ring.tile([P, S], F32, name="feat", tag="feat", bufs=2)
            nc.scalar.activation(feats[0][:, cols], wg_plain[:, cols], ACT.Copy, scale=gn_first[:])
            squash(0, half, b1_first[:])

        def put_first_features(half):
            cols = slice(half * BANK, (half + 1) * BANK)
            nc.vector.tensor_tensor(
                pages[0][:].indirect(half_of(idx2, half)), squashed[0][:, cols], feats[0][:, cols], ALU.mult
            )

        def features(s):
            if s < PACK:
                b1 = b1_plain[:, s - 1 : s]
            else:
                b1 = b1_dealt[:, LANES[s - PACK] : LANES[s - PACK] + 1]
            new_squashed(s)
            for half in range(HALVES):
                squash(s, half, b1)
            feats[s] = ring.tile([P, S], F32, name="feat", tag="feat", bufs=2)
            nc.scalar.activation(feats[s][:], squashed[s][:], ACT.Copy, scale=gains[s][:])

        def put_features(s):
            wg = wg_plain[:] if s < PACK else wg_dealt[LANES[s - PACK]]
            nc.vector.tensor_tensor(pages[s][:].indirect(idx2[:]), feats[s][:], wg, ALU.mult)

        pair = {}

        def fetch_pairs(s, first=None, second=None):
            if first is None:
                first = ring.tile([P, PAIRS], F32, name="first", tag="first", bufs=2)[:]
            if second is None:
                second = ring.tile([P, PAIRS], F32, name="second", tag="second", bufs=2)[:]
            nc.vector.tensor_copy(first, pages[s][:].indirect(idx3[:]))
            nc.vector.tensor_copy(second, pages[s][:].indirect(idx4[:]))
            pair[s] = (first, second)

        def order_pairs(s):
            first, second = pair[s]
            if s + 1 == SLICES:
                new_squashed(SLICES)
            larger, smaller = squashed[s + 1][:, 0:PAIRS], squashed[s + 1][:, PAIRS : 2 * PAIRS]
            nc.vector.tensor_tensor(larger, first, second, ALU.max)
            nc.vector.tensor_tensor(smaller, first, second, ALU.min)
            pair[s] = (larger, smaller)

        def put_larger(s):
            nc.vector.tensor_copy(pages[s][:].indirect(idx3[:]), pair[s][0])

        def put_smaller(s, ordered):
            nc.vector.tensor_copy(pages[s][:].indirect(idx4[:]), ordered[1])

        board_woven = {}
        board_mx = {}
        planes = {}
        sums = {}
        staged = {}

        def new_woven(b, c):
            board_woven[b, c] = ring.tile(
                [P, BANK, PACK], BF16, name="board_woven", tag=f"{('woven', 'planes')[b]}{c}", bufs=1, align_bytes=64
            )

        def round_and_deal(s):
            rounded = ring.tile([P, T2], BF16, name="rounded", tag="rounded", bufs=1)
            nc.scalar.copy(rounded[:], pages[s][:])
            for c in range(CHUNKS):
                if s == 0:
                    planes[c] = ring.tile([P, PACK, BANK], BF16, name="planes", tag=f"planes{c}", bufs=1, align_bytes=64)
                nc.scalar.dma_start(planes[c][QUAD * s : QUAD * (s + 1), :, :], rounded[:, c * BANK : (c + 1) * BANK])

        def weave_planes(c):
            new_woven(0, c)
            nc.scalar.copy(board_woven[0, c][:], planes[c][:].rearrange("p t c -> p c t"))

        def weave_page(s, c):
            if s == PACK:
                new_woven(1, c)
            copy = nc.vector.tensor_copy if s == SLICES - 1 else nc.scalar.copy
            copy(board_woven[1, c][:, :, LANES[s - PACK]], pages[s][:, c * BANK : (c + 1) * BANK])

        def quantize_board(b, c):
            tag = f"codes1{c}" if b == 1 else ("first_spent", "second_spent", "woven0", "woven1")[c]
            codes = ring.tile([P, BANK], U32, name="board_codes", tag=tag, bufs=1, align_bytes=64)
            scales = held.tile([P, BANK], U8, name=f"board_scales{b}{c}", align_bytes=64)
            nc.vector.quantize_mx(
                out=codes[:].bitcast(FP8X4), scales=scales[:], in_=board_woven[b, c][:].rearrange("p c t -> p (c t)")
            )
            board_mx[b, c] = (codes, scales)

        def read_out(b, c, m, start, stop):
            codes, scales = board_mx[b, c]
            if start:
                sums[c, m] = psum.tile([P, BANK], F32, name="acc", tag="bank")
            nc.tensor.matmul_mx(
                out=sums[c, m][:],
                lhsT=w4w[:, b, 2 * P * m : 2 * P * (m + 1)].bitcast(FP4X4),
                lhsT_scale=w4s[:, b, P * m : P * (m + 1)],
                rhs=codes[:].bitcast(FP8X4),
                rhs_scale=scales[:],
                start=start,
                stop=stop,
            )

        def finish(c, m):
            if m == 0:
                staged[c] = ring.tile([P, NTILES, BANK], F32, name="staged", tag="raw", bufs=4)
            if m == 0 or (c == CHUNKS - 1 and m < NTILES - 1):
                nc.vector.tensor_scalar_add(staged[c][:, m, :], sums[c, m][:], b2[:, m : m + 1])
            else:
                nc.scalar.activation(staged[c][:, m, :], sums[c, m][:], ACT.Identity, bias=b2[:, m : m + 1])
            nc.sync.dma_start(out[m * P : (m + 1) * P, c * BANK : (c + 1) * BANK], staged[c][:, m, :])

        both = (0, 1)
        early = 2
        gather_words(0, 0)
        gather_scales(0)
        gather_words(0, 1)
        gather_words(1, 0)
        for a in both:
            weave_w1((a,), 0, P, f"woven_first{a}")
        for a in both:
            quantize_w1((a,), 0, P)
        first_features(0)
        gather_scales(1)
        gather_words(1, 1)
        put_first_features(0)
        weave_w1(both, P, 2 * P, "woven1")
        first_features(1)
        quantize_w1(both, P, 2 * P)
        put_first_features(1)
        weave_w1(both, 2 * P, PASS, "woven0")
        features(1)
        quantize_w1(both, 2 * P, PASS)
        fetch_pairs(
            0, w1_woven[both, P].bitcast(F32)[:, 0:PAIRS], w1_woven[both, 2 * P].bitcast(F32)[:, 0:PAIRS]
        )
        for a in both:
            weave_w1((a,), PASS, H, f"woven{2 + a}")

        for s in range(SLICES):
            last = s == SLICES - 1
            if s + 2 < SLICES:
                features(s + 2)
            if not last:
                put_features(s + 1)
            order_pairs(s)
            put_larger(s)
            if s == 1:
                for a in both:
                    quantize_w1((a,), PASS, H)
                fetch_pairs(s + 1, w1_woven[(1,), PASS].bitcast(F32)[:, 0:PAIRS])
            elif s == PACK + 1:
                for c in range(CHUNKS):
                    quantize_board(0, c)
                    if c < early:
                        for m in range(NTILES):
                            read_out(0, c, m, True, False)
                spent = board_woven[0, CHUNKS - 1][:].rearrange("p c t -> p (c t)").bitcast(F32)
                fetch_pairs(s + 1, None, spent[:, 0:PAIRS])
            elif s == PACK:
                first = ring.tile([P, PAIRS], F32, name="first", tag="first_spent", bufs=1, align_bytes=64)
                second = ring.tile([P, PAIRS], F32, name="second", tag="second_spent", bufs=1, align_bytes=64)
                fetch_pairs(s + 1, first[:], second[:])
            elif not last:
                fetch_pairs(s + 1)
            put_smaller(s, pair[s])
            if s < PACK:
                round_and_deal(s)
            if s == PACK:
                for c in range(CHUNKS):
                    weave_planes(c)
            if PACK <= s and not last:
                for c in range(CHUNKS):
                    weave_page(s, c)
        for c in range(CHUNKS):
            weave_page(SLICES - 1, c)
            quantize_board(1, c)
            for m in range(NTILES):
                if c >= early:
                    read_out(0, c, m, True, False)
                read_out(1, c, m, False, True)
                finish(c, m)
